import numpy as np
import ml_dtypes


def mxq(x, axis, fmt="e4m3"):
    dtype, down = {"e4m3": (ml_dtypes.float8_e4m3fn, 7), "e5m2": (ml_dtypes.float8_e5m2, 14)}[fmt]
    v = np.moveaxis(np.asarray(x, np.float32).astype(ml_dtypes.bfloat16).astype(np.float64), axis, -1)
    blocks = v.reshape(v.shape[:-1] + (-1, 32))
    amax = np.abs(blocks).max(-1, keepdims=True)
    byte = np.maximum(np.where(amax > 0, np.frexp(amax)[1] - 1 + 127, 0) - down, 1)
    scale = np.exp2(byte - 127.0)
    codes = (blocks / scale).astype(np.float32).astype(dtype).astype(np.float64)
    return np.moveaxis((codes * scale).reshape(v.shape), -1, axis)


WIDE = False


def mx_kscale(k):
    if not WIDE:
        return np.ones(k)
    levels = np.array([10, -10, 5, -5, 0])
    if k % 512:
        return np.exp2(np.random.permutation(np.resize(levels, k // 32))).repeat(32)
    a = np.empty((k // 512, 16))
    for p in range(k // 512):
        a[p, :8] = np.random.permutation(np.resize(levels, 8))
        for g in range(8):
            far = levels[np.abs(levels - a[p, g]) >= 10]
            a[p, g + 8] = far[np.random.randint(len(far))]
    return np.exp2(a.ravel()).repeat(32)


def f64(x):
    return np.asarray(x).astype(np.float64)


def striped(idx):
    return np.tile(idx.reshape(-1, 16).T, (8, 1)).astype(np.uint16)


def unstriped(offs):
    return offs[:16].T.reshape(-1).astype(np.int64)


K, T, E, C, N = 512, 512, 4, 128, 128


def by_expert(wq, xq):
    return np.concatenate([wq[e].T @ xq[:, e * C:(e + 1) * C] for e in range(E)], axis=1)


def setup_inputs():
    n = np.random.standard_normal
    s = mx_kscale(K)[:, None]
    return {
        "xT": (n((K, T)) * s).astype(np.float32),
        "w": (n((E, K, N)) / np.sqrt(K) / s[None]).astype(np.float32),
        "offs": striped(np.random.permutation(T)[:E * C]),
    }


def reference(xT, w, offs):
    idx = unstriped(offs)
    xq = mxq(f64(xT)[:, idx], 0, "e4m3")
    y = by_expert(mxq(f64(w), 1, "e4m3"), xq)
    out = np.zeros((N, T))
    out[:, idx] = y
    return out

@@ -1,0 +1,110 @@
+from contextlib import ExitStack
+
+import concourse.mybir as mybir
+
+K, T, E, C, N = 512, 512, 4, 128, 128
+FLOPS = 2 * K * N * E * C
+
+F32 = mybir.dt.float32
+BF16 = mybir.dt.bfloat16
+U32 = mybir.dt.uint32
+U16 = mybir.dt.uint16
+U8 = mybir.dt.uint8
+FP8X4 = mybir.dt.float8_e4m3fn_x4
+
+P = 128
+HALF = 256
+LIST_COLS = HALF // 16
+
+
+def tile_routed_moe_kernel(tc, xT, w, offs, out):
+    nc = tc.nc
+    with ExitStack() as ctx:
+        keep = ctx.enter_context(tc.tile_pool(name="keep", bufs=1))
+        psum = ctx.enter_context(tc.psum_pool(name="psum", bufs=1))
+
+        offsets = keep.tile([P, E * C // 16], U16, name="offsets")
+
+        x_view = xT.rearrange("(p u e) n -> p u e n", u=2, e=2)
+        raw_x = []
+        for u in range(2):
+            t = keep.tile([P, 2, T], F32, name="raw_x%d" % u)
+            nc.sync.dma_start(t[:], x_view[:, u])
+            raw_x.append(t)
+            if u == 0:
+                nc.sync.dma_start(offsets[:], offs)
+        w_view = w.rearrange("e (p t) n -> p e t n", t=4)
+        raw_w = []
+        for h in range(2):
+            t = keep.tile([P, 2, 4, N], F32, name="raw_w%d" % h)
+            nc.sync.dma_start(t[:], w_view[:, 2 * h : 2 * h + 2])
+            raw_w.append(t)
+
+        pairs = []
+        for u in range(2):
+            t = keep.tile([P, T, 2], BF16, name="pairs%d" % u)
+            src = raw_x[u][:].rearrange("p e n -> p n e")
+            if u == 0:
+                nc.vector.tensor_copy(out=t[:, 0:336, :], in_=src[:, 0:336, :])
+                nc.scalar.copy(out=t[:, 336:T, :], in_=src[:, 336:T, :])
+            else:
+                nc.scalar.copy(out=t[:], in_=src)
+            pairs.append(t)
+
+        w_codes, w_scales = [], []
+        x_codes, x_scales = [], []
+        grouped = []
+        for h in range(2):
+            g = keep.tile([P, HALF, 4], BF16, name="grouped%d" % h, align_bytes=64)
+            grouped.append(g)
+        for u in range(2):
+            window = pairs[u][:].rearrange("p n e -> p (n e)").bitcast(U32)
+            for h in range(2):
+                words = grouped[h][:].rearrange("p s t -> p (s t)").bitcast(U32).rearrange("p (s u) -> p s u", u=2)
+                nc.vector.tensor_copy(
+                    out=words[:, :, u],
+                    in_=window.indirect(offsets[:, h * LIST_COLS : (h + 1) * LIST_COLS]),
+                )
+
+        for h in range(2):
+            wg = keep.tile([P, 2, N, 4], BF16, name="w_grouped%d" % h, align_bytes=64)
+            for j in range(2):
+                nc.scalar.copy(
+                    out=wg[:, j].rearrange("p (c i) t -> p c t i", i=4),
+                    in_=raw_w[h][:, j].rearrange("p t (c i) -> p c t i", i=4),
+                )
+            wc = keep.tile([P, 2 * N], U32, name="w_codes%d" % h, align_bytes=64)
+            ws = keep.tile([P, 2 * N], U8, name="w_scales%d" % h, align_bytes=64)
+            nc.vector.quantize_mx(
+                out=wc[:].bitcast(FP8X4), scales=ws[:], in_=wg[:].rearrange("p e n t -> p (e n t)")
+            )
+            w_codes.append(wc)
+            w_scales.append(ws)
+            xc = keep.tile([P, HALF], U32, name="x_codes%d" % h, align_bytes=64)
+            xs = keep.tile([P, HALF], U8, name="x_scales%d" % h, align_bytes=64)
+            nc.vector.quantize_mx(
+                out=xc[:].bitcast(FP8X4), scales=xs[:], in_=grouped[h][:].rearrange("p s t -> p (s t)")
+            )
+            x_codes.append(xc)
+            x_scales.append(xs)
+
+        result = keep.tile([P, T], F32, name="result")
+        for h in range(2):
+            acc = psum.tile([P, HALF], F32, name="acc%d" % h)
+            for j in range(2):
+                cols = slice(j * C, (j + 1) * C)
+                nc.tensor.matmul_mx(
+                    out=acc[:, cols],
+                    lhsT=w_codes[h][:, cols].bitcast(FP8X4),
+                    lhsT_scale=w_scales[h][:, cols],
+                    rhs=x_codes[h][:, cols].bitcast(FP8X4),
+                    rhs_scale=x_scales[h][:, cols],
+                    start=True,
+                    stop=True,
+                )
+            y = keep.tile([P, HALF], F32, name="y%d" % h)
+            nc.scalar.copy(out=y[:], in_=acc[:])
+            nc.vector.tensor_copy(
+                out=result[:].indirect(offsets[:, h * LIST_COLS : (h + 1) * LIST_COLS]), in_=y[:]
+            )
+        nc.sync.dma_start(out, result[:])

@@ -15,6 +15,8 @@ FP8X4 = mybir.dt.float8_e4m3fn_x4
 P = 128
 HALF = 256
 LIST_COLS = HALF // 16
+CHUNK = 256
+VSHARE = 160
 
 
 def tile_routed_moe_kernel(tc, xT, w, offs, out):
@@ -28,27 +30,32 @@ def tile_routed_moe_kernel(tc, xT, w, offs, out):
         x_view = xT.rearrange("(p u e) n -> p u e n", u=2, e=2)
         raw_x = []
         for u in range(2):
-            t = keep.tile([P, 2, T], F32, name="raw_x%d" % u)
-            nc.sync.dma_start(t[:], x_view[:, u])
-            raw_x.append(t)
+            for c in range(2):
+                t = keep.tile([P, 2, CHUNK], F32, name="raw_x%d%d" % (u, c))
+                nc.sync.dma_start(t[:], x_view[:, u, :, c * CHUNK : (c + 1) * CHUNK])
+                raw_x.append(t)
             if u == 0:
                 nc.sync.dma_start(offsets[:], offs)
-        w_view = w.rearrange("e (p t) n -> p e t n", t=4)
+        w_view = w.rearrange("e (p t) n -> e p t n", t=4)
         raw_w = []
-        for h in range(2):
-            t = keep.tile([P, 2, 4, N], F32, name="raw_w%d" % h)
-            nc.sync.dma_start(t[:], w_view[:, 2 * h : 2 * h + 2])
+        for e in range(E):
+            t = keep.tile([P, 4, N], F32, name="raw_w%d" % e)
+            nc.sync.dma_start(t[:], w_view[e])
             raw_w.append(t)
 
         pairs = []
         for u in range(2):
             t = keep.tile([P, T, 2], BF16, name="pairs%d" % u)
-            src = raw_x[u][:].rearrange("p e n -> p n e")
-            if u == 0:
-                nc.vector.tensor_copy(out=t[:, 0:336, :], in_=src[:, 0:336, :])
-                nc.scalar.copy(out=t[:, 336:T, :], in_=src[:, 336:T, :])
-            else:
-                nc.scalar.copy(out=t[:], in_=src)
+            for c in range(2):
+                src = raw_x[2 * u + c][:].rearrange("p e n -> p n e")
+                dst = t[:, c * CHUNK : (c + 1) * CHUNK, :]
+                if u == 0 and c == 0:
+                    nc.vector.tensor_copy(out=dst, in_=src)
+                elif u == 0:
+                    nc.vector.tensor_copy(out=dst[:, 0:VSHARE, :], in_=src[:, 0:VSHARE, :])
+                    nc.scalar.copy(out=dst[:, VSHARE:CHUNK, :], in_=src[:, VSHARE:CHUNK, :])
+                else:
+                    nc.scalar.copy(out=dst, in_=src)
             pairs.append(t)
 
         w_codes, w_scales = [], []
@@ -71,7 +78,7 @@ def tile_routed_moe_kernel(tc, xT, w, offs, out):
             for j in range(2):
                 nc.scalar.copy(
                     out=wg[:, j].rearrange("p (c i) t -> p c t i", i=4),
-                    in_=raw_w[h][:, j].rearrange("p t (c i) -> p c t i", i=4),
+                    in_=raw_w[2 * h + j][:].rearrange("p t (c i) -> p c t i", i=4),
                 )
             wc = keep.tile([P, 2 * N], U32, name="w_codes%d" % h, align_bytes=64)
             ws = keep.tile([P, 2 * N], U8, name="w_scales%d" % h, align_bytes=64)

@@ -8,6 +8,7 @@ FLOPS = 2 * K * N * E * C
 F32 = mybir.dt.float32
 BF16 = mybir.dt.bfloat16
 U32 = mybir.dt.uint32
+I32 = mybir.dt.int32
 U16 = mybir.dt.uint16
 U8 = mybir.dt.uint8
 FP8X4 = mybir.dt.float8_e4m3fn_x4
@@ -58,35 +59,43 @@ def tile_routed_moe_kernel(tc, xT, w, offs, out):
                     nc.scalar.copy(out=dst, in_=src)
             pairs.append(t)
 
-        w_codes, w_scales = [], []
-        x_codes, x_scales = [], []
         grouped = []
         for h in range(2):
             g = keep.tile([P, HALF, 4], BF16, name="grouped%d" % h, align_bytes=64)
             grouped.append(g)
-        for u in range(2):
-            window = pairs[u][:].rearrange("p n e -> p (n e)").bitcast(U32)
-            for h in range(2):
-                words = grouped[h][:].rearrange("p s t -> p (s t)").bitcast(U32).rearrange("p (s u) -> p s u", u=2)
-                nc.vector.tensor_copy(
-                    out=words[:, :, u],
-                    in_=window.indirect(offsets[:, h * LIST_COLS : (h + 1) * LIST_COLS]),
-                )
 
-        for h in range(2):
+        def gather(u, h):
+            window = pairs[u][:].rearrange("p n e -> p (n e)").bitcast(U32)
+            words = grouped[h][:].rearrange("p s t -> p (s t)").bitcast(U32).rearrange("p (s u) -> p s u", u=2)
+            nc.vector.tensor_copy(
+                out=words[:, :, u],
+                in_=window.indirect(offsets[:, h * LIST_COLS : (h + 1) * LIST_COLS]),
+            )
+
+        w_grouped = []
+
+        def cast_w(h):
             wg = keep.tile([P, 2, N, 4], BF16, name="w_grouped%d" % h, align_bytes=64)
             for j in range(2):
                 nc.scalar.copy(
                     out=wg[:, j].rearrange("p (c i) t -> p c t i", i=4),
                     in_=raw_w[2 * h + j][:].rearrange("p t (c i) -> p c t i", i=4),
                 )
+            w_grouped.append(wg)
+
+        w_codes, w_scales = [], []
+        x_codes, x_scales = [], []
+
+        def quantize_w(h):
             wc = keep.tile([P, 2 * N], U32, name="w_codes%d" % h, align_bytes=64)
             ws = keep.tile([P, 2 * N], U8, name="w_scales%d" % h, align_bytes=64)
             nc.vector.quantize_mx(
-                out=wc[:].bitcast(FP8X4), scales=ws[:], in_=wg[:].rearrange("p e n t -> p (e n t)")
+                out=wc[:].bitcast(FP8X4), scales=ws[:], in_=w_grouped[h][:].rearrange("p e n t -> p (e n t)")
             )
             w_codes.append(wc)
             w_scales.append(ws)
+
+        def quantize_x(h):
             xc = keep.tile([P, HALF], U32, name="x_codes%d" % h, align_bytes=64)
             xs = keep.tile([P, HALF], U8, name="x_scales%d" % h, align_bytes=64)
             nc.vector.quantize_mx(
@@ -94,6 +103,19 @@ def tile_routed_moe_kernel(tc, xT, w, offs, out):
             )
             x_codes.append(xc)
             x_scales.append(xs)
+
+        gather(0, 0)
+        gather(0, 1)
+        gather(1, 0)
+        quantize_x(0)
+        cast_w(0)
+        quantize_w(0)
+        late = grouped[1][:].rearrange("p s t -> p (s t)").bitcast(I32)
+        nc.vector.tensor_copy(out=late[:, 1:2], in_=x_codes[0][:, 0:1].bitcast(I32))
+        gather(1, 1)
+        quantize_x(1)
+        cast_w(1)
+        quantize_w(1)
 
         result = keep.tile([P, T], F32, name="result")
         for h in range(2):

@@ -8,7 +8,6 @@ FLOPS = 2 * K * N * E * C
 F32 = mybir.dt.float32
 BF16 = mybir.dt.bfloat16
 U32 = mybir.dt.uint32
-I32 = mybir.dt.int32
 U16 = mybir.dt.uint16
 U8 = mybir.dt.uint8
 FP8X4 = mybir.dt.float8_e4m3fn_x4
@@ -17,6 +16,7 @@ P = 128
 HALF = 256
 LIST_COLS = HALF // 16
 CHUNK = 256
+PAD = 176
 VSHARE = 160
 
 
@@ -46,7 +46,9 @@ def tile_routed_moe_kernel(tc, xT, w, offs, out):
 
         pairs = []
         for u in range(2):
-            t = keep.tile([P, T, 2], BF16, name="pairs%d" % u)
+            t = keep.tile([P, T + PAD * (1 - u), 2], BF16, name="pairs%d" % u)
+            if u == 0:
+                nc.gpsimd.memset(t[:, T : T + PAD, :], 0.0)
             for c in range(2):
                 src = raw_x[2 * u + c][:].rearrange("p e n -> p n e")
                 dst = t[:, c * CHUNK : (c + 1) * CHUNK, :]
@@ -59,17 +61,14 @@ def tile_routed_moe_kernel(tc, xT, w, offs, out):
                     nc.scalar.copy(out=dst, in_=src)
             pairs.append(t)
 
-        grouped = []
-        for h in range(2):
-            g = keep.tile([P, HALF, 4], BF16, name="grouped%d" % h, align_bytes=64)
-            grouped.append(g)
+        grouped = keep.tile([P, 2 * HALF, 4], BF16, name="grouped", align_bytes=64)
+        words = grouped[:].rearrange("p s t -> p (s t)").bitcast(U32).rearrange("p (s u) -> p s u", u=2)
 
-        def gather(u, h):
+        def gather(u, first, count):
             window = pairs[u][:].rearrange("p n e -> p (n e)").bitcast(U32)
-            words = grouped[h][:].rearrange("p s t -> p (s t)").bitcast(U32).rearrange("p (s u) -> p s u", u=2)
             nc.vector.tensor_copy(
-                out=words[:, :, u],
-                in_=window.indirect(offsets[:, h * LIST_COLS : (h + 1) * LIST_COLS]),
+                out=words[:, first : first + count, u],
+                in_=window.indirect(offsets[:, first // 16 : (first + count) // 16]),
             )
 
         w_grouped = []
@@ -99,20 +98,18 @@ def tile_routed_moe_kernel(tc, xT, w, offs, out):
             xc = keep.tile([P, HALF], U32, name="x_codes%d" % h, align_bytes=64)
             xs = keep.tile([P, HALF], U8, name="x_scales%d" % h, align_bytes=64)
             nc.vector.quantize_mx(
-                out=xc[:].bitcast(FP8X4), scales=xs[:], in_=grouped[h][:].rearrange("p s t -> p (s t)")
+                out=xc[:].bitcast(FP8X4), scales=xs[:], in_=grouped[:, h * HALF : (h + 1) * HALF, :].rearrange("p s t -> p (s t)")
             )
             x_codes.append(xc)
             x_scales.append(xs)
 
-        gather(0, 0)
-        gather(0, 1)
-        gather(1, 0)
+        gather(0, 0, 2 * HALF)
+        gather(1, 0, HALF)
         quantize_x(0)
         cast_w(0)
         quantize_w(0)
-        late = grouped[1][:].rearrange("p s t -> p (s t)").bitcast(I32)
-        nc.vector.tensor_copy(out=late[:, 1:2], in_=x_codes[0][:, 0:1].bitcast(I32))
-        gather(1, 1)
+        nc.scalar.copy(out=grouped[:, HALF, 2:4], in_=w_grouped[0][:, 1, N - 1, 2:4])
+        gather(1, HALF, HALF)
         quantize_x(1)
         cast_w(1)
         quantize_w(1)

@@ -17,7 +17,6 @@ HALF = 256
 LIST_COLS = HALF // 16
 CHUNK = 256
 PAD = 176
-VSHARE = 160
 
 
 def tile_routed_moe_kernel(tc, xT, w, offs, out):
@@ -52,11 +51,8 @@ def tile_routed_moe_kernel(tc, xT, w, offs, out):
             for c in range(2):
                 src = raw_x[2 * u + c][:].rearrange("p e n -> p n e")
                 dst = t[:, c * CHUNK : (c + 1) * CHUNK, :]
-                if u == 0 and c == 0:
+                if u == 0:
                     nc.vector.tensor_copy(out=dst, in_=src)
-                elif u == 0:
-                    nc.vector.tensor_copy(out=dst[:, 0:VSHARE, :], in_=src[:, 0:VSHARE, :])
-                    nc.scalar.copy(out=dst[:, VSHARE:CHUNK, :], in_=src[:, VSHARE:CHUNK, :])
                 else:
                     nc.scalar.copy(out=dst, in_=src)
             pairs.append(t)

@@ -69,46 +69,49 @@ def tile_routed_moe_kernel(tc, xT, w, offs, out):
 
         w_grouped = []
 
-        def cast_w(h):
-            wg = keep.tile([P, 2, N, 4], BF16, name="w_grouped%d" % h, align_bytes=64)
-            for j in range(2):
-                nc.scalar.copy(
-                    out=wg[:, j].rearrange("p (c i) t -> p c t i", i=4),
-                    in_=raw_w[2 * h + j][:].rearrange("p t (c i) -> p c t i", i=4),
-                )
+        def cast_w(e):
+            wg = keep.tile([P, N, 4], BF16, name="w_grouped%d" % e, align_bytes=64)
+            nc.scalar.copy(
+                out=wg[:].rearrange("p (c i) t -> p c t i", i=4),
+                in_=raw_w[e][:].rearrange("p t (c i) -> p c t i", i=4),
+            )
             w_grouped.append(wg)
 
         w_codes, w_scales = [], []
         x_codes, x_scales = [], []
 
-        def quantize_w(h):
-            wc = keep.tile([P, 2 * N], U32, name="w_codes%d" % h, align_bytes=64)
-            ws = keep.tile([P, 2 * N], U8, name="w_scales%d" % h, align_bytes=64)
-            nc.vector.quantize_mx(
-                out=wc[:].bitcast(FP8X4), scales=ws[:], in_=w_grouped[h][:].rearrange("p e n t -> p (e n t)")
+        def w_operand(e):
+            w_codes.append(keep.tile([P, N], U32, name="w_codes%d" % e, align_bytes=64))
+            w_scales.append(keep.tile([P, N], U8, name="w_scales%d" % e, align_bytes=64))
+            return dict(
+                out=w_codes[e][:].bitcast(FP8X4),
+                scales=w_scales[e][:],
+                in_=w_grouped[e][:].rearrange("p n t -> p (n t)"),
             )
-            w_codes.append(wc)
-            w_scales.append(ws)
 
-        def quantize_x(h):
-            xc = keep.tile([P, HALF], U32, name="x_codes%d" % h, align_bytes=64)
-            xs = keep.tile([P, HALF], U8, name="x_scales%d" % h, align_bytes=64)
-            nc.vector.quantize_mx(
-                out=xc[:].bitcast(FP8X4), scales=xs[:], in_=grouped[:, h * HALF : (h + 1) * HALF, :].rearrange("p s t -> p (s t)")
+        def x_operand(h):
+            x_codes.append(keep.tile([P, HALF], U32, name="x_codes%d" % h, align_bytes=64))
+            x_scales.append(keep.tile([P, HALF], U8, name="x_scales%d" % h, align_bytes=64))
+            return dict(
+                out=x_codes[h][:].bitcast(FP8X4),
+                scales=x_scales[h][:],
+                in_=grouped[:, h * HALF : (h + 1) * HALF, :].rearrange("p s t -> p (s t)"),
             )
-            x_codes.append(xc)
-            x_scales.append(xs)
 
         gather(0, 0, 2 * HALF)
         gather(1, 0, HALF)
-        quantize_x(0)
         cast_w(0)
-        quantize_w(0)
-        nc.scalar.copy(out=grouped[:, HALF, 2:4], in_=w_grouped[0][:, 1, N - 1, 2:4])
-        gather(1, HALF, HALF)
-        quantize_x(1)
+        nc.vector.quantize_mx(**w_operand(0))
+        nc.vector.quantize_mx(**x_operand(0))
         cast_w(1)
-        quantize_w(1)
+        nc.vector.quantize_mx(**w_operand(1))
+        nc.scalar.copy(out=grouped[:, HALF, 2:4], in_=w_grouped[1][:, N - 1, 2:4])
+        gather(1, HALF, HALF)
+        cast_w(2)
+        nc.vector.quantize_mx(**w_operand(2))
+        nc.vector.quantize_mx(**x_operand(1))
+        cast_w(3)
+        nc.vector.quantize_mx(**w_operand(3))
 
         result = keep.tile([P, T], F32, name="result")
         for h in range(2):
@@ -117,8 +120,8 @@ def tile_routed_moe_kernel(tc, xT, w, offs, out):
                 cols = slice(j * C, (j + 1) * C)
                 nc.tensor.matmul_mx(
                     out=acc[:, cols],
-                    lhsT=w_codes[h][:, cols].bitcast(FP8X4),
-                    lhsT_scale=w_scales[h][:, cols],
+                    lhsT=w_codes[2 * h + j][:].bitcast(FP8X4),
+                    lhsT_scale=w_scales[2 * h + j][:],
                     rhs=x_codes[h][:, cols].bitcast(FP8X4),
                     rhs_scale=x_scales[h][:, cols],
                     start=True,

@@ -70,7 +70,7 @@ def tile_routed_moe_kernel(tc, xT, w, offs, out):
         w_grouped = []
 
         def cast_w(e):
-            wg = keep.tile([P, N, 4], BF16, name="w_grouped%d" % e, align_bytes=64)
+            wg = keep.tile([P, N, 4], BF16, name="w_grouped%d" % e, tag="turn%d" % e, align_bytes=64)
             nc.scalar.copy(
                 out=wg[:].rearrange("p (c i) t -> p c t i", i=4),
                 in_=raw_w[e][:].rearrange("p t (c i) -> p c t i", i=4),
@@ -90,7 +90,7 @@ def tile_routed_moe_kernel(tc, xT, w, offs, out):
             )
 
         def x_operand(h):
-            x_codes.append(keep.tile([P, HALF], U32, name="x_codes%d" % h, align_bytes=64))
+            x_codes.append(keep.tile([P, HALF], U32, name="x_codes%d" % h, tag="turn%d" % (2 * h), align_bytes=64))
             x_scales.append(keep.tile([P, HALF], U8, name="x_scales%d" % h, align_bytes=64))
             return dict(
                 out=x_codes[h][:].bitcast(FP8X4),
@@ -105,7 +105,7 @@ def tile_routed_moe_kernel(tc, xT, w, offs, out):
         nc.vector.quantize_mx(**x_operand(0))
         cast_w(1)
         nc.vector.quantize_mx(**w_operand(1))
-        nc.scalar.copy(out=grouped[:, HALF, 2:4], in_=w_grouped[1][:, N - 1, 2:4])
+        nc.scalar.copy(out=grouped[:, HALF, 2:4], in_=raw_w[1][:, 0, 0:2])
         gather(1, HALF, HALF)
         cast_w(2)
         nc.vector.quantize_mx(**w_operand(2))

@@ -90,7 +90,8 @@ def tile_routed_moe_kernel(tc, xT, w, offs, out):
             )
 
         def x_operand(h):
-            x_codes.append(keep.tile([P, HALF], U32, name="x_codes%d" % h, tag="turn%d" % (2 * h), align_bytes=64))
+            tag = ("turn0", "x_codes1")[h]
+            x_codes.append(keep.tile([P, HALF], U32, name="x_codes%d" % h, tag=tag, align_bytes=64))
             x_scales.append(keep.tile([P, HALF], U8, name="x_scales%d" % h, align_bytes=64))
             return dict(
                 out=x_codes[h][:].bitcast(FP8X4),
@@ -115,11 +116,12 @@ def tile_routed_moe_kernel(tc, xT, w, offs, out):
 
         result = keep.tile([P, T], F32, name="result")
         for h in range(2):
-            acc = psum.tile([P, HALF], F32, name="acc%d" % h)
+            y = keep.tile([P, HALF], F32, name="y%d" % h)
             for j in range(2):
                 cols = slice(j * C, (j + 1) * C)
+                acc = psum.tile([P, C], F32, name="acc%d" % (2 * h + j))
                 nc.tensor.matmul_mx(
-                    out=acc[:, cols],
+                    out=acc[:],
                     lhsT=w_codes[2 * h + j][:].bitcast(FP8X4),
                     lhsT_scale=w_scales[2 * h + j][:],
                     rhs=x_codes[h][:, cols].bitcast(FP8X4),
@@ -127,8 +129,7 @@ def tile_routed_moe_kernel(tc, xT, w, offs, out):
                     start=True,
                     stop=True,
                 )
-            y = keep.tile([P, HALF], F32, name="y%d" % h)
-            nc.scalar.copy(out=y[:], in_=acc[:])
+                nc.scalar.copy(out=y[:, cols], in_=acc[:])
             nc.vector.tensor_copy(
                 out=result[:].indirect(offsets[:, h * LIST_COLS : (h + 1) * LIST_COLS]), in_=y[:]
             )

from contextlib import ExitStack

import concourse.mybir as mybir

K, T, E, C, N = 512, 512, 4, 128, 128
FLOPS = 2 * K * N * E * C

F32 = mybir.dt.float32
BF16 = mybir.dt.bfloat16
U32 = mybir.dt.uint32
U16 = mybir.dt.uint16
U8 = mybir.dt.uint8
FP8X4 = mybir.dt.float8_e4m3fn_x4

P = 128
HALF = 256
LIST_COLS = HALF // 16
CHUNK = 256
PAD = 176


def tile_routed_moe_kernel(tc, xT, w, offs, out):
    nc = tc.nc
    with ExitStack() as ctx:
        keep = ctx.enter_context(tc.tile_pool(name="keep", bufs=1))
        psum = ctx.enter_context(tc.psum_pool(name="psum", bufs=1))

        offsets = keep.tile([P, E * C // 16], U16, name="offsets")

        x_view = xT.rearrange("(p u e) n -> p u e n", u=2, e=2)
        raw_x = []
        for u in range(2):
            for c in range(2):
                t = keep.tile([P, 2, CHUNK], F32, name="raw_x%d%d" % (u, c))
                nc.sync.dma_start(t[:], x_view[:, u, :, c * CHUNK : (c + 1) * CHUNK])
                raw_x.append(t)
            if u == 0:
                nc.sync.dma_start(offsets[:], offs)
        w_view = w.rearrange("e (p t) n -> e p t n", t=4)
        raw_w = []
        for e in range(E):
            t = keep.tile([P, 4, N], F32, name="raw_w%d" % e)
            nc.sync.dma_start(t[:], w_view[e])
            raw_w.append(t)

        pairs = []
        for u in range(2):
            t = keep.tile([P, T + PAD * (1 - u), 2], BF16, name="pairs%d" % u)
            if u == 0:
                nc.gpsimd.memset(t[:, T : T + PAD, :], 0.0)
            for c in range(2):
                src = raw_x[2 * u + c][:].rearrange("p e n -> p n e")
                dst = t[:, c * CHUNK : (c + 1) * CHUNK, :]
                if u == 0:
                    nc.vector.tensor_copy(out=dst, in_=src)
                else:
                    nc.scalar.copy(out=dst, in_=src)
            pairs.append(t)

        grouped = keep.tile([P, 2 * HALF, 4], BF16, name="grouped", align_bytes=64)
        words = grouped[:].rearrange("p s t -> p (s t)").bitcast(U32).rearrange("p (s u) -> p s u", u=2)

        def gather(u, first, count):
            window = pairs[u][:].rearrange("p n e -> p (n e)").bitcast(U32)
            nc.vector.tensor_copy(
                out=words[:, first : first + count, u],
                in_=window.indirect(offsets[:, first // 16 : (first + count) // 16]),
            )

        w_grouped = []

        def cast_w(e):
            wg = keep.tile([P, N, 4], BF16, name="w_grouped%d" % e, tag="turn%d" % e, align_bytes=64)
            nc.scalar.copy(
                out=wg[:].rearrange("p (c i) t -> p c t i", i=4),
                in_=raw_w[e][:].rearrange("p t (c i) -> p c t i", i=4),
            )
            w_grouped.append(wg)

        w_codes, w_scales = [], []
        x_codes, x_scales = [], []

        def w_operand(e):
            w_codes.append(keep.tile([P, N], U32, name="w_codes%d" % e, align_bytes=64))
            w_scales.append(keep.tile([P, N], U8, name="w_scales%d" % e, align_bytes=64))
            return dict(
                out=w_codes[e][:].bitcast(FP8X4),
                scales=w_scales[e][:],
                in_=w_grouped[e][:].rearrange("p n t -> p (n t)"),
            )

        def x_operand(h):
            tag = ("turn0", "x_codes1")[h]
            x_codes.append(keep.tile([P, HALF], U32, name="x_codes%d" % h, tag=tag, align_bytes=64))
            x_scales.append(keep.tile([P, HALF], U8, name="x_scales%d" % h, align_bytes=64))
            return dict(
                out=x_codes[h][:].bitcast(FP8X4),
                scales=x_scales[h][:],
                in_=grouped[:, h * HALF : (h + 1) * HALF, :].rearrange("p s t -> p (s t)"),
            )

        gather(0, 0, 2 * HALF)
        gather(1, 0, HALF)
        cast_w(0)
        nc.vector.quantize_mx(**w_operand(0))
        nc.vector.quantize_mx(**x_operand(0))
        cast_w(1)
        nc.vector.quantize_mx(**w_operand(1))
        nc.scalar.copy(out=grouped[:, HALF, 2:4], in_=raw_w[1][:, 0, 0:2])
        gather(1, HALF, HALF)
        cast_w(2)
        nc.vector.quantize_mx(**w_operand(2))
        nc.vector.quantize_mx(**x_operand(1))
        cast_w(3)
        nc.vector.quantize_mx(**w_operand(3))

        result = keep.tile([P, T], F32, name="result")
        for h in range(2):
            y = keep.tile([P, HALF], F32, name="y%d" % h)
            for j in range(2):
                cols = slice(j * C, (j + 1) * C)
                acc = psum.tile([P, C], F32, name="acc%d" % (2 * h + j))
                nc.tensor.matmul_mx(
                    out=acc[:],
                    lhsT=w_codes[2 * h + j][:].bitcast(FP8X4),
                    lhsT_scale=w_scales[2 * h + j][:],
                    rhs=x_codes[h][:, cols].bitcast(FP8X4),
                    rhs_scale=x_scales[h][:, cols],
                    start=True,
                    stop=True,
                )
                nc.scalar.copy(out=y[:, cols], in_=acc[:])
            nc.vector.tensor_copy(
                out=result[:].indirect(offsets[:, h * LIST_COLS : (h + 1) * LIST_COLS]), in_=y[:]
            )
        nc.sync.dma_start(out, result[:])
